import numpy as np, ml_dtypes
CORES = [122,123,126,250,251,254,378,379,382,506,507,510]
N = 12
KB, QP = 1, 128
def setup_inputs(rng):
    q = rng.standard_normal((N, 128, QP), dtype=np.float32) / 4; k = rng.standard_normal((N, 128, KB * 128), dtype=np.float32)
    a = 2 * np.pi * rng.random((N, QP)); s = 400 * rng.random((N, QP)) ** 1.5; q[:, 0, :] = s * np.cos(a); q[:, 1, :] = s * np.sin(a); q[:, 2, :] = 150 * rng.standard_normal((N, QP)); k[:, 2, :] = 1 + k[:, 2, :] / 50
    a = (2 * np.pi * rng.random() + np.pi / 2 * (rng.permutation(N).reshape(N, 1, 1) + 0.5) / N - 0.5 + (np.arange(KB).reshape(1, KB, 1) + rng.random((N, KB, 128))) / KB).reshape(N, KB * 128); k[:, 0, :] = np.cos(a); k[:, 1, :] = np.sin(a)
    return {"q": q.astype(ml_dtypes.bfloat16), "k": k.astype(ml_dtypes.bfloat16), "v": rng.standard_normal((N, 128, KB * 128), dtype=np.float32).astype(ml_dtypes.bfloat16)}
def setup_inputs_big(rng):
    d = setup_inputs(rng)
    for k in ("v",): d[k] = (d[k].astype(np.float32) * 1048576.0).astype(d[k].dtype)
    return d
def setup_inputs_small(rng):
    d = setup_inputs(rng)
    for k in ("v",): d[k] = (d[k].astype(np.float32) * (1 / 1048576.0)).astype(d[k].dtype)
    return d
def reference(q, k, v):
    Q, K, V = q.astype(np.float64), k.astype(np.float64), v.astype(np.float64)
    y = np.zeros((N, QP, 128))
    for r in range(N):
        js = list(range(r + 1))
        S = np.concatenate([K[j].T @ Q[r] for j in js], axis=0)
        kp = np.concatenate([j * KB * 128 + np.arange(KB * 128) for j in js]); S = np.where(kp[:, None] <= (r * QP + np.arange(QP))[None, :], S, -np.inf)
        P = np.exp(S - S.max(axis=0)); P = P / P.sum(axis=0)
        y[r] = P.T @ np.concatenate([V[j][:, 128 * b:128 * b + 128] for j in js for b in range(KB)], axis=0)
    return {"y": y.astype(ml_dtypes.bfloat16)}

@@ -1,0 +1,264 @@
+from concourse.bass import DstId, RemoteDMATransfer
+from concourse.mybir import AluOpType, AxisListType, ActivationFunctionType
+
+B = 128
+SW = 264
+NSLOT = 6
+NEV = 48
+BIG = -30000.0
+
+SCRATCH = {
+    "kv": ("sbuf", [128, NSLOT * SW], "bfloat16"),
+    "qo": ("sbuf", [128, B], "bfloat16"),
+    "qf": ("sbuf", [128, B], "bfloat16"),
+    "dd": ("sbuf", [128, B], "bfloat16"),
+    "zm": ("sbuf", [128, B], "bfloat16"),
+    "mb": ("sbuf", [128, B], "bfloat16"),
+    "ident": ("sbuf", [128, B], "bfloat16"),
+    "ee": ("sbuf", [128, B], "bfloat16"),
+    "p": ("sbuf", [128, 4 * 3 * B], "bfloat16"),
+    "pts": ("sbuf", [128, 4 * 3 * B], "bfloat16"),
+    "mx": ("sbuf", [128, 4], "float32"),
+    "negc": ("sbuf", [128, 1], "float32"),
+    "dcol": ("sbuf", [128, 1], "float32"),
+    "rcol": ("sbuf", [128, 1], "float32"),
+    "ret": ("sbuf", [128, B + 2], "bfloat16"),
+    "retin": ("sbuf", [128, B + 2], "bfloat16"),
+    "ysb": ("sbuf", [128, B], "bfloat16"),
+    "sa": ("psum", [128, 512], "float32"),
+    "sb": ("psum", [128, 512], "float32"),
+    "sx": ("psum", [128, 512], "float32"),
+    "sy": ("psum", [128, 512], "float32"),
+    "pta": ("psum", [128, 1024], "bfloat16"),
+    "ptb": ("psum", [128, 1024], "bfloat16"),
+    "outf": ("psum", [128, 512], "float32"),
+    "outo": ("psum", [128, 512], "float32"),
+}
+SEMAPHORES = ["ld_kv", "ld_q", "kv_on", "kv_off", "q_in", "p_in", "sent", "st"] + ["e%d" % i for i in range(NEV)]
+
+
+def rank_program(g, core, T, topo):
+    rank = T.rank_of(core)
+    if rank is None:
+        return
+    EXP = ActivationFunctionType.Exp
+    X = AxisListType.X
+    Q = {"pe": g.tensor, "dve": g.vector, "act": g.scalar, "sync": g.sync, "g": g}
+
+    cores = list(T.cores)
+
+    def place(c):
+        return (topo.host(c), topo.chip(c))
+
+    def rack(c):
+        return topo.rack(topo.host(c))
+
+    lower = [c for c in cores if rack(c) == rack(cores[0])]
+    upper = [c for c in cores if rack(c) != rack(cores[0])]
+
+    def idx_on_chip(c):
+        return [d for d in cores if place(d) == place(c)].index(c)
+
+    def partner_of(u):
+        for l in lower:
+            if idx_on_chip(l) == idx_on_chip(u) and topo.may_write(u, l) and topo.may_write(l, u):
+                return l
+        return None
+
+    is_low = core in lower
+    mine = lower if is_low else upper
+    rr = mine.index(core)
+    on = [j for j in range(len(mine)) if place(mine[j]) == place(core)]
+    off = [j for j in range(len(mine)) if place(mine[j]) != place(core)]
+    far = [u for u in upper if partner_of(u) == core][0] if is_low else partner_of(core)
+
+    def bits(m):
+        return bin(m).count("1")
+
+    m_off = topo.mask(core, far)
+    m_on = topo.mask(core, mine[[j for j in on if j != rr][0]]) & ~m_off
+
+    ctr = [0]
+    waited = {}
+
+    def ev(sem=None, n=0):
+        ctr[0] += 1
+        if sem is None:
+            sem = T.sem["e%d" % (ctr[0] - 1)]
+        return [sem, n, ctr[0]]
+
+    def sig(ins, e, n=1):
+        ins.then_inc(e[0], n)
+        e[1] += n
+
+    def wt(qn, *es):
+        for e in es:
+            if e[1] > 0 and waited.get((qn, e[2])) != e[1]:
+                Q[qn].wait_ge(e[0], e[1])
+                waited[(qn, e[2])] = e[1]
+
+    def slot(j, a, b):
+        return T.kv[:, j * SW + a:j * SW + b]
+
+    takers = [j for j in range(len(mine)) if j != rr and (is_low or j > rr)]
+    givers = [j for j in range(len(mine)) if j != rr and (is_low or j < rr)]
+    ld_kv, ld_q = ev(T.sem.ld_kv), ev(T.sem.ld_q)
+    kv_on = ev(T.sem.kv_on, bits(m_on) * len([j for j in givers if j in on]))
+    kv_off = ev(T.sem.kv_off, bits(m_off) * len([j for j in givers if j in off]))
+    q_in = ev(T.sem.q_in, bits(m_off) if is_low else 0)
+    p_in = ev(T.sem.p_in, 0 if is_low else bits(m_off))
+    sent, st = ev(T.sem.sent), ev(T.sem.st)
+
+    if is_low:
+        sig(g.sync.dma_start(slot(rr, 0, B), T.k[:]), ld_kv, 16)
+        sig(g.scalar.dma_start(slot(rr, B, 2 * B), T.v[:]), ld_kv, 16)
+        sig(g.sync.dma_start(T.qo[:], T.q[:]), ld_q, 16)
+    else:
+        sig(g.sync.dma_start(T.qo[:], T.q[:]), ld_q, 16)
+        sig(g.scalar.dma_start(slot(rr, 0, B), T.k[:]), ld_kv, 16)
+        sig(g.sync.dma_start(slot(rr, B, 2 * B), T.v[:]), ld_kv, 16)
+
+    e_dd, e_zm, e_mb, e_id, e_one = ev(), ev(), ev(), ev(), ev()
+    sig(g.iota(T.dd[:], [[-1, B]], 0, 1, allow_small_or_imprecise_dtypes=True), e_dd)
+    for j in sorted(set(givers + [rr])):
+        sig(g.vector.memset(slot(j, 2 * B, 2 * B + 8), 1.0), e_one)
+    wt("dve", e_dd)
+    sig(g.vector.tensor_scalar(T.zm[:], T.dd[:], 0.0, BIG, AluOpType.not_equal, AluOpType.mult), e_zm)
+    sig(g.vector.tensor_scalar(T.mb[:], T.dd[:], 0.0, BIG, AluOpType.is_lt, AluOpType.mult), e_mb)
+    wt("act", e_zm)
+    sig(g.scalar.activation(T.ident[:], T.zm[:], EXP), e_id)
+
+    def send(src, dst, dests, mask, rsem):
+        ids = []
+        for d in dests:
+            rid, pid = topo.addr(d, core)
+            ids.append(DstId(rid=rid, pnc=pid))
+        tr = RemoteDMATransfer(dst_ids=ids, dma_engine_mask=mask, remote_sem=rsem, srcs=[src],
+                               dsts=[dst for d in dests], alu_op=0)
+        g.remote_dma_fused([tr], local_sem=sent[0])
+        sent[1] += bits(mask)
+
+    if not is_low:
+        wt("g", ld_q)
+        send(T.qo[:], T.qf[:], [far], m_off, T.sem.q_in)
+    wt("g", ld_kv)
+    t_off = [mine[j] for j in takers if j in off]
+    t_on = [mine[j] for j in takers if j in on]
+    if t_off:
+        send(slot(rr, 0, 2 * B), slot(rr, 0, 2 * B), t_off, m_off, T.sem.kv_off)
+    if t_on:
+        send(slot(rr, 0, 2 * B), slot(rr, 0, 2 * B), t_on, m_on, T.sem.kv_on)
+
+    def chunk(slots, s, pt, k, is_on):
+        data = [kv_on] if is_on else [kv_off]
+        if rr in slots:
+            data = data + [ld_kv]
+        return {"slots": slots, "s": s, "pt": pt, "o": k * 3 * B, "n": len(slots) * B, "data": data, "k": k,
+                "S": ev(), "M": ev(), "E": ev(), "T": ev(), "C": ev()}
+
+    def st_S(J, c):
+        wt("pe", *(J["qe"] + c["data"]))
+        for b, j in enumerate(c["slots"]):
+            o = c["s"][:, b * B:(b + 1) * B]
+            if J["causal"] and j == rr:
+                wt("pe", e_id, e_mb)
+                g.tensor.matmul(o, J["q"], slot(j, 0, B), True, False)
+                sig(g.tensor.matmul(o, T.ident[:], T.mb[:], False, True), c["S"])
+            else:
+                sig(g.tensor.matmul(o, J["q"], slot(j, 0, B), True, True), c["S"])
+
+    def st_max(J, c):
+        wt("dve", c["S"])
+        if len(J["chunks"]) == 1:
+            sig(g.vector.tensor_reduce(J["negm"], c["s"][:, 0:c["n"]], X, AluOpType.max, negate=True), J["N"])
+        else:
+            sig(g.vector.tensor_reduce(T.mx[:, c["k"]:c["k"] + 1], c["s"][:, 0:c["n"]], X, AluOpType.max), c["M"])
+
+    def st_comb(J):
+        if len(J["chunks"]) > 1:
+            wt("dve", *[c["M"] for c in J["chunks"]])
+            k0 = J["chunks"][0]["k"]
+            sig(g.vector.tensor_reduce(J["negm"], T.mx[:, k0:k0 + 2], X, AluOpType.max, negate=True), J["N"])
+
+    def st_exp(J, c):
+        wt("act", J["N"], c["S"])
+        sig(g.scalar.activation(T.p[:, c["o"]:c["o"] + c["n"]], c["s"][:, 0:c["n"]], EXP, bias=J["negm"], scale=1.0), c["E"])
+
+    def st_T(J, c):
+        wt("pe", c["E"], e_id)
+        for b in range(len(c["slots"])):
+            sig(g.tensor.transpose(c["pt"][:, b * B:(b + 1) * B], T.p[:, c["o"] + b * B:c["o"] + (b + 1) * B], T.ident[:]), c["T"])
+
+    def st_copy(J, c):
+        wt("dve", c["T"])
+        sig(g.vector.tensor_copy(T.pts[:, c["o"]:c["o"] + c["n"]], c["pt"][:, 0:c["n"]]), c["C"])
+
+    def st_PV(J, c, close):
+        wt("pe", c["C"], e_one, *c["data"])
+        first = c is J["chunks"][0]
+        last = c is J["chunks"][-1]
+        for b, j in enumerate(c["slots"]):
+            sig(g.tensor.matmul(J["out"][:, 0:B + 1], T.pts[:, c["o"] + b * B:c["o"] + (b + 1) * B], slot(j, B, 2 * B + 1),
+                                first and b == 0, close and last and b == len(c["slots"]) - 1), J["P"])
+
+    def st_y(J):
+        e_r, e_y = ev(), ev()
+        wt("dve", J["P"])
+        sig(g.vector.reciprocal(T.rcol[:], J["out"][:, B:B + 1]), e_r)
+        wt("dve", e_r)
+        sig(g.vector.tensor_scalar(T.ysb[:], J["out"][:, 0:B], T.rcol[:], None, AluOpType.mult), e_y)
+        wt("sync", e_y)
+        sig(g.sync.dma_start(T.y[:], T.ysb[:]), st, 16)
+        wt("sync", st)
+
+    C = {"q": T.qo[:], "qe": [ld_q], "causal": True, "out": T.outo, "negm": T.negc[:], "N": ev(), "P": ev()}
+    C["chunks"] = [chunk([j for j in on if j <= rr], T.sx, T.pta, 2, True)]
+    if [j for j in off if j <= rr]:
+        C["chunks"].append(chunk([j for j in off if j <= rr], T.sy, T.ptb, 3, False))
+    cc = C["chunks"]
+
+    if is_low:
+        F = {"q": T.qf[:], "qe": [q_in], "causal": False, "out": T.outf, "negm": T.ret[:, B + 1:B + 2], "N": ev(), "P": ev()}
+        F["chunks"] = [chunk(on, T.sa, T.pta, 0, True), chunk(off, T.sb, T.ptb, 1, False)]
+        fa, fb = F["chunks"]
+        st_S(C, cc[0]); st_max(C, cc[0])
+        st_S(F, fa); st_max(F, fa)
+        st_S(F, fb); st_max(F, fb); st_comb(F)
+        for c in cc[1:]:
+            st_S(C, c)
+        st_exp(F, fa); st_exp(F, fb)
+        for c in cc[1:]:
+            st_max(C, c)
+        st_comb(C)
+        st_T(F, fa); st_T(F, fb)
+        st_copy(F, fa); st_copy(F, fb)
+        st_PV(F, fa, True); st_PV(F, fb, True)
+        e_ret = ev()
+        wt("dve", F["P"])
+        sig(g.vector.tensor_copy(T.ret[:, 0:B + 1], T.outf[:, 0:B + 1]), e_ret)
+        wt("g", e_ret, F["N"])
+        send(T.ret[:], T.retin[:], [far], m_off, T.sem.p_in)
+    else:
+        for c in cc:
+            st_S(C, c); st_max(C, c)
+        st_comb(C)
+
+    for c in cc:
+        st_exp(C, c)
+    for c in cc:
+        st_T(C, c)
+    for c in cc:
+        st_copy(C, c)
+    for c in cc:
+        st_PV(C, c, is_low)
+
+    if not is_low:
+        e_d, e_e = ev(), ev()
+        wt("dve", p_in, C["N"])
+        sig(g.vector.tensor_scalar(T.dcol[:], T.negc[:], T.retin[:, B + 1:B + 2], 60.0, AluOpType.subtract, AluOpType.min), e_d)
+        wt("act", e_d, e_zm)
+        sig(g.scalar.activation(T.ee[:], T.zm[:], EXP, bias=T.dcol[:], scale=1.0), e_e)
+        wt("pe", e_e, p_in)
+        sig(g.tensor.matmul(T.outo[:, 0:B + 1], T.ee[:], T.retin[:, 0:B + 1], False, True), C["P"])
+    st_y(C)
+    wt("g", sent)

@@ -3,8 +3,10 @@ from concourse.mybir import AluOpType, AxisListType, ActivationFunctionType
 
 B = 128
 SW = 264
-NSLOT = 6
-NEV = 48
+NSLOT = 7
+FAR = 6
+CW = 4 * B
+NEV = 72
 BIG = -30000.0
 
 SCRATCH = {
@@ -16,14 +18,16 @@ SCRATCH = {
     "mb": ("sbuf", [128, B], "bfloat16"),
     "ident": ("sbuf", [128, B], "bfloat16"),
     "ee": ("sbuf", [128, B], "bfloat16"),
-    "p": ("sbuf", [128, 4 * 3 * B], "bfloat16"),
-    "pts": ("sbuf", [128, 4 * 3 * B], "bfloat16"),
+    "p": ("sbuf", [128, 4 * CW], "bfloat16"),
+    "pts": ("sbuf", [128, 4 * CW], "bfloat16"),
     "mx": ("sbuf", [128, 4], "float32"),
     "negc": ("sbuf", [128, 1], "float32"),
+    "nm": ("sbuf", [128, 1], "float32"),
+    "nmin": ("sbuf", [128, 1], "float32"),
     "dcol": ("sbuf", [128, 1], "float32"),
     "rcol": ("sbuf", [128, 1], "float32"),
-    "ret": ("sbuf", [128, B + 2], "bfloat16"),
-    "retin": ("sbuf", [128, B + 2], "bfloat16"),
+    "ret": ("sbuf", [128, B + 1], "bfloat16"),
+    "retin": ("sbuf", [128, B + 1], "bfloat16"),
     "ysb": ("sbuf", [128, B], "bfloat16"),
     "sa": ("psum", [128, 512], "float32"),
     "sb": ("psum", [128, 512], "float32"),
@@ -34,7 +38,8 @@ SCRATCH = {
     "outf": ("psum", [128, 512], "float32"),
     "outo": ("psum", [128, 512], "float32"),
 }
-SEMAPHORES = ["ld_kv", "ld_q", "kv_on", "kv_off", "q_in", "p_in", "sent", "st"] + ["e%d" % i for i in range(NEV)]
+SEMAPHORES = ["ld_kv", "ld_v", "ld_q", "kv_on", "kv_off", "v_off", "kv_far", "q_in", "m_in", "p_in", "sent", "st"] \
+    + ["e%d" % i for i in range(NEV)]
 
 
 def rank_program(g, core, T, topo):
@@ -75,8 +80,11 @@ def rank_program(g, core, T, topo):
     def bits(m):
         return bin(m).count("1")
 
-    m_off = topo.mask(core, far)
-    m_on = topo.mask(core, mine[[j for j in on if j != rr][0]]) & ~m_off
+    m_all = topo.mask(core, far)
+    m_on = topo.mask(core, mine[[j for j in on if j != rr][0]]) & ~m_all
+    leave = [i for i in range(m_all.bit_length()) if (m_all >> i) & 1]
+    m_sw = sum([1 << i for i in leave[0::2]])
+    m_cb = sum([1 << i for i in leave[1::2]])
 
     ctr = [0]
     waited = {}
@@ -102,25 +110,28 @@ def rank_program(g, core, T, topo):
 
     takers = [j for j in range(len(mine)) if j != rr and (is_low or j > rr)]
     givers = [j for j in range(len(mine)) if j != rr and (is_low or j < rr)]
-    ld_kv, ld_q = ev(T.sem.ld_kv), ev(T.sem.ld_q)
+    ld_kv, ld_v, ld_q = ev(T.sem.ld_kv), ev(T.sem.ld_v), ev(T.sem.ld_q)
     kv_on = ev(T.sem.kv_on, bits(m_on) * len([j for j in givers if j in on]))
-    kv_off = ev(T.sem.kv_off, bits(m_off) * len([j for j in givers if j in off]))
-    q_in = ev(T.sem.q_in, bits(m_off) if is_low else 0)
-    p_in = ev(T.sem.p_in, 0 if is_low else bits(m_off))
+    kv_off = ev(T.sem.kv_off, bits(m_sw) * len([j for j in givers if j in off]))
+    v_off = ev(T.sem.v_off, kv_off[1]) if is_low else kv_off
+    kv_far = ev(T.sem.kv_far, 0 if is_low else bits(m_cb))
+    q_in = ev(T.sem.q_in, bits(m_cb) if is_low else 0)
+    m_in = ev(T.sem.m_in, 0 if is_low else bits(m_cb))
+    p_in = ev(T.sem.p_in, 0 if is_low else bits(m_cb))
     sent, st = ev(T.sem.sent), ev(T.sem.st)
 
     if is_low:
         sig(g.sync.dma_start(slot(rr, 0, B), T.k[:]), ld_kv, 16)
-        sig(g.scalar.dma_start(slot(rr, B, 2 * B), T.v[:]), ld_kv, 16)
+        sig(g.scalar.dma_start(slot(rr, B, 2 * B), T.v[:]), ld_v, 16)
         sig(g.sync.dma_start(T.qo[:], T.q[:]), ld_q, 16)
     else:
         sig(g.sync.dma_start(T.qo[:], T.q[:]), ld_q, 16)
         sig(g.scalar.dma_start(slot(rr, 0, B), T.k[:]), ld_kv, 16)
-        sig(g.sync.dma_start(slot(rr, B, 2 * B), T.v[:]), ld_kv, 16)
+        sig(g.sync.dma_start(slot(rr, B, 2 * B), T.v[:]), ld_v, 16)
 
     e_dd, e_zm, e_mb, e_id, e_one = ev(), ev(), ev(), ev(), ev()
     sig(g.iota(T.dd[:], [[-1, B]], 0, 1, allow_small_or_imprecise_dtypes=True), e_dd)
-    for j in sorted(set(givers + [rr])):
+    for j in sorted(set(givers + [rr])) + ([] if is_low else [FAR]):
         sig(g.vector.memset(slot(j, 2 * B, 2 * B + 8), 1.0), e_one)
     wt("dve", e_dd)
     sig(g.vector.tensor_scalar(T.zm[:], T.dd[:], 0.0, BIG, AluOpType.not_equal, AluOpType.mult), e_zm)
@@ -140,21 +151,27 @@ def rank_program(g, core, T, topo):
 
     if not is_low:
         wt("g", ld_q)
-        send(T.qo[:], T.qf[:], [far], m_off, T.sem.q_in)
-    wt("g", ld_kv)
+        send(T.qo[:], T.qf[:], [far], m_cb, T.sem.q_in)
     t_off = [mine[j] for j in takers if j in off]
     t_on = [mine[j] for j in takers if j in on]
-    if t_off:
-        send(slot(rr, 0, 2 * B), slot(rr, 0, 2 * B), t_off, m_off, T.sem.kv_off)
+    wt("g", ld_kv)
+    if is_low:
+        send(slot(rr, 0, B), slot(rr, 0, B), t_off, m_sw, T.sem.kv_off)
+    wt("g", ld_v)
+    if t_off and not is_low:
+        send(slot(rr, 0, 2 * B), slot(rr, 0, 2 * B), t_off, m_sw, T.sem.kv_off)
     if t_on:
         send(slot(rr, 0, 2 * B), slot(rr, 0, 2 * B), t_on, m_on, T.sem.kv_on)
+    if is_low:
+        send(slot(rr, 0, 2 * B), slot(FAR, 0, 2 * B), [far], m_cb, T.sem.kv_far)
+        send(slot(rr, B, 2 * B), slot(rr, B, 2 * B), t_off, m_sw, T.sem.v_off)
 
-    def chunk(slots, s, pt, k, is_on):
-        data = [kv_on] if is_on else [kv_off]
+    def chunk(slots, s, pt, k, data, vdata):
         if rr in slots:
             data = data + [ld_kv]
-        return {"slots": slots, "s": s, "pt": pt, "o": k * 3 * B, "n": len(slots) * B, "data": data, "k": k,
-                "S": ev(), "M": ev(), "E": ev(), "T": ev(), "C": ev()}
+            vdata = vdata + [ld_v]
+        return {"slots": slots, "s": s, "pt": pt, "o": k * CW, "n": len(slots) * B, "data": data, "vdata": vdata, "k": k,
+                "S": ev(), "M": ev(), "E": [ev() for j in slots], "T": ev(), "C": ev()}
 
     def st_S(J, c):
         wt("pe", *(J["qe"] + c["data"]))
@@ -182,11 +199,14 @@ def rank_program(g, core, T, topo):
 
     def st_exp(J, c):
         wt("act", J["N"], c["S"])
-        sig(g.scalar.activation(T.p[:, c["o"]:c["o"] + c["n"]], c["s"][:, 0:c["n"]], EXP, bias=J["negm"], scale=1.0), c["E"])
+        for b in range(len(c["slots"])):
+            sig(g.scalar.activation(T.p[:, c["o"] + b * B:c["o"] + (b + 1) * B], c["s"][:, b * B:(b + 1) * B], EXP,
+                                    bias=J["negm"], scale=1.0), c["E"][b])
 
     def st_T(J, c):
-        wt("pe", c["E"], e_id)
+        wt("pe", e_id)
         for b in range(len(c["slots"])):
+            wt("pe", c["E"][b])
             sig(g.tensor.transpose(c["pt"][:, b * B:(b + 1) * B], T.p[:, c["o"] + b * B:c["o"] + (b + 1) * B], T.ident[:]), c["T"])
 
     def st_copy(J, c):
@@ -194,7 +214,7 @@ def rank_program(g, core, T, topo):
         sig(g.vector.tensor_copy(T.pts[:, c["o"]:c["o"] + c["n"]], c["pt"][:, 0:c["n"]]), c["C"])
 
     def st_PV(J, c, close):
-        wt("pe", c["C"], e_one, *c["data"])
+        wt("pe", c["C"], e_one, *c["vdata"])
         first = c is J["chunks"][0]
         last = c is J["chunks"][-1]
         for b, j in enumerate(c["slots"]):
@@ -212,18 +232,22 @@ def rank_program(g, core, T, topo):
         wt("sync", st)
 
     C = {"q": T.qo[:], "qe": [ld_q], "causal": True, "out": T.outo, "negm": T.negc[:], "N": ev(), "P": ev()}
-    C["chunks"] = [chunk([j for j in on if j <= rr], T.sx, T.pta, 2, True)]
-    if [j for j in off if j <= rr]:
-        C["chunks"].append(chunk([j for j in off if j <= rr], T.sy, T.ptb, 3, False))
+    C["chunks"] = [chunk([j for j in on if j <= rr], T.sx, T.pta, 2, [kv_on], [kv_on])]
+    second = [j for j in off if j <= rr] + ([] if is_low else [FAR])
+    if second:
+        C["chunks"].append(chunk(second, T.sy, T.ptb, 3, [kv_off, kv_far], [v_off, kv_far]))
     cc = C["chunks"]
 
     if is_low:
-        F = {"q": T.qf[:], "qe": [q_in], "causal": False, "out": T.outf, "negm": T.ret[:, B + 1:B + 2], "N": ev(), "P": ev()}
-        F["chunks"] = [chunk(on, T.sa, T.pta, 0, True), chunk(off, T.sb, T.ptb, 1, False)]
+        F = {"q": T.qf[:], "qe": [q_in], "causal": False, "out": T.outf, "negm": T.nm[:], "N": ev(), "P": ev()}
+        F["chunks"] = [chunk([j for j in on if j != rr], T.sa, T.pta, 0, [kv_on], [kv_on]),
+                       chunk(off, T.sb, T.ptb, 1, [kv_off], [v_off])]
         fa, fb = F["chunks"]
         st_S(C, cc[0]); st_max(C, cc[0])
         st_S(F, fa); st_max(F, fa)
         st_S(F, fb); st_max(F, fb); st_comb(F)
+        wt("g", F["N"])
+        send(T.nm[:], T.nmin[:], [far], m_cb, T.sem.m_in)
         for c in cc[1:]:
             st_S(C, c)
         st_exp(F, fa); st_exp(F, fb)
@@ -235,9 +259,9 @@ def rank_program(g, core, T, topo):
         st_PV(F, fa, True); st_PV(F, fb, True)
         e_ret = ev()
         wt("dve", F["P"])
-        sig(g.vector.tensor_copy(T.ret[:, 0:B + 1], T.outf[:, 0:B + 1]), e_ret)
-        wt("g", e_ret, F["N"])
-        send(T.ret[:], T.retin[:], [far], m_off, T.sem.p_in)
+        sig(g.vector.tensor_copy(T.ret[:], T.outf[:, 0:B + 1]), e_ret)
+        wt("g", e_ret)
+        send(T.ret[:], T.retin[:], [far], m_cb, T.sem.p_in)
     else:
         for c in cc:
             st_S(C, c); st_max(C, c)
@@ -254,11 +278,11 @@ def rank_program(g, core, T, topo):
 
     if not is_low:
         e_d, e_e = ev(), ev()
-        wt("dve", p_in, C["N"])
-        sig(g.vector.tensor_scalar(T.dcol[:], T.negc[:], T.retin[:, B + 1:B + 2], 60.0, AluOpType.subtract, AluOpType.min), e_d)
+        wt("dve", m_in, C["N"])
+        sig(g.vector.tensor_scalar(T.dcol[:], T.negc[:], T.nmin[:], 60.0, AluOpType.subtract, AluOpType.min), e_d)
         wt("act", e_d, e_zm)
         sig(g.scalar.activation(T.ee[:], T.zm[:], EXP, bias=T.dcol[:], scale=1.0), e_e)
         wt("pe", e_e, p_in)
-        sig(g.tensor.matmul(T.outo[:, 0:B + 1], T.ee[:], T.retin[:, 0:B + 1], False, True), C["P"])
+        sig(g.tensor.matmul(T.outo[:, 0:B + 1], T.ee[:], T.retin[:], False, True), C["P"])
     st_y(C)
     wt("g", sent)

from concourse.bass import DstId, RemoteDMATransfer
from concourse.mybir import AluOpType, AxisListType, ActivationFunctionType

B = 128
SW = 264
NSLOT = 7
FAR = 6
CW = 4 * B
NEV = 72
BIG = -30000.0

SCRATCH = {
    "kv": ("sbuf", [128, NSLOT * SW], "bfloat16"),
    "qo": ("sbuf", [128, B], "bfloat16"),
    "qf": ("sbuf", [128, B], "bfloat16"),
    "dd": ("sbuf", [128, B], "bfloat16"),
    "zm": ("sbuf", [128, B], "bfloat16"),
    "mb": ("sbuf", [128, B], "bfloat16"),
    "ident": ("sbuf", [128, B], "bfloat16"),
    "ee": ("sbuf", [128, B], "bfloat16"),
    "p": ("sbuf", [128, 4 * CW], "bfloat16"),
    "pts": ("sbuf", [128, 4 * CW], "bfloat16"),
    "mx": ("sbuf", [128, 4], "float32"),
    "negc": ("sbuf", [128, 1], "float32"),
    "nm": ("sbuf", [128, 1], "float32"),
    "nmin": ("sbuf", [128, 1], "float32"),
    "dcol": ("sbuf", [128, 1], "float32"),
    "rcol": ("sbuf", [128, 1], "float32"),
    "ret": ("sbuf", [128, B + 1], "bfloat16"),
    "retin": ("sbuf", [128, B + 1], "bfloat16"),
    "ysb": ("sbuf", [128, B], "bfloat16"),
    "sa": ("psum", [128, 512], "float32"),
    "sb": ("psum", [128, 512], "float32"),
    "sx": ("psum", [128, 512], "float32"),
    "sy": ("psum", [128, 512], "float32"),
    "pta": ("psum", [128, 1024], "bfloat16"),
    "ptb": ("psum", [128, 1024], "bfloat16"),
    "outf": ("psum", [128, 512], "float32"),
    "outo": ("psum", [128, 512], "float32"),
}
SEMAPHORES = ["ld_kv", "ld_v", "ld_q", "kv_on", "kv_off", "v_off", "kv_far", "q_in", "m_in", "p_in", "sent", "st"] \
    + ["e%d" % i for i in range(NEV)]


def rank_program(g, core, T, topo):
    rank = T.rank_of(core)
    if rank is None:
        return
    EXP = ActivationFunctionType.Exp
    X = AxisListType.X
    Q = {"pe": g.tensor, "dve": g.vector, "act": g.scalar, "sync": g.sync, "g": g}

    cores = list(T.cores)

    def place(c):
        return (topo.host(c), topo.chip(c))

    def rack(c):
        return topo.rack(topo.host(c))

    lower = [c for c in cores if rack(c) == rack(cores[0])]
    upper = [c for c in cores if rack(c) != rack(cores[0])]

    def idx_on_chip(c):
        return [d for d in cores if place(d) == place(c)].index(c)

    def partner_of(u):
        for l in lower:
            if idx_on_chip(l) == idx_on_chip(u) and topo.may_write(u, l) and topo.may_write(l, u):
                return l
        return None

    is_low = core in lower
    mine = lower if is_low else upper
    rr = mine.index(core)
    on = [j for j in range(len(mine)) if place(mine[j]) == place(core)]
    off = [j for j in range(len(mine)) if place(mine[j]) != place(core)]
    far = [u for u in upper if partner_of(u) == core][0] if is_low else partner_of(core)

    def bits(m):
        return bin(m).count("1")

    m_all = topo.mask(core, far)
    m_on = topo.mask(core, mine[[j for j in on if j != rr][0]]) & ~m_all
    leave = [i for i in range(m_all.bit_length()) if (m_all >> i) & 1]
    m_sw = sum([1 << i for i in leave[0::2]])
    m_cb = sum([1 << i for i in leave[1::2]])

    ctr = [0]
    waited = {}

    def ev(sem=None, n=0):
        ctr[0] += 1
        if sem is None:
            sem = T.sem["e%d" % (ctr[0] - 1)]
        return [sem, n, ctr[0]]

    def sig(ins, e, n=1):
        ins.then_inc(e[0], n)
        e[1] += n

    def wt(qn, *es):
        for e in es:
            if e[1] > 0 and waited.get((qn, e[2])) != e[1]:
                Q[qn].wait_ge(e[0], e[1])
                waited[(qn, e[2])] = e[1]

    def slot(j, a, b):
        return T.kv[:, j * SW + a:j * SW + b]

    takers = [j for j in range(len(mine)) if j != rr and (is_low or j > rr)]
    givers = [j for j in range(len(mine)) if j != rr and (is_low or j < rr)]
    ld_kv, ld_v, ld_q = ev(T.sem.ld_kv), ev(T.sem.ld_v), ev(T.sem.ld_q)
    kv_on = ev(T.sem.kv_on, bits(m_on) * len([j for j in givers if j in on]))
    kv_off = ev(T.sem.kv_off, bits(m_sw) * len([j for j in givers if j in off]))
    v_off = ev(T.sem.v_off, kv_off[1]) if is_low else kv_off
    kv_far = ev(T.sem.kv_far, 0 if is_low else bits(m_cb))
    q_in = ev(T.sem.q_in, bits(m_cb) if is_low else 0)
    m_in = ev(T.sem.m_in, 0 if is_low else bits(m_cb))
    p_in = ev(T.sem.p_in, 0 if is_low else bits(m_cb))
    sent, st = ev(T.sem.sent), ev(T.sem.st)

    if is_low:
        sig(g.sync.dma_start(slot(rr, 0, B), T.k[:]), ld_kv, 16)
        sig(g.scalar.dma_start(slot(rr, B, 2 * B), T.v[:]), ld_v, 16)
        sig(g.sync.dma_start(T.qo[:], T.q[:]), ld_q, 16)
    else:
        sig(g.sync.dma_start(T.qo[:], T.q[:]), ld_q, 16)
        sig(g.scalar.dma_start(slot(rr, 0, B), T.k[:]), ld_kv, 16)
        sig(g.sync.dma_start(slot(rr, B, 2 * B), T.v[:]), ld_v, 16)

    e_dd, e_zm, e_mb, e_id, e_one = ev(), ev(), ev(), ev(), ev()
    sig(g.iota(T.dd[:], [[-1, B]], 0, 1, allow_small_or_imprecise_dtypes=True), e_dd)
    for j in sorted(set(givers + [rr])) + ([] if is_low else [FAR]):
        sig(g.vector.memset(slot(j, 2 * B, 2 * B + 8), 1.0), e_one)
    wt("dve", e_dd)
    sig(g.vector.tensor_scalar(T.zm[:], T.dd[:], 0.0, BIG, AluOpType.not_equal, AluOpType.mult), e_zm)
    sig(g.vector.tensor_scalar(T.mb[:], T.dd[:], 0.0, BIG, AluOpType.is_lt, AluOpType.mult), e_mb)
    wt("act", e_zm)
    sig(g.scalar.activation(T.ident[:], T.zm[:], EXP), e_id)

    def send(src, dst, dests, mask, rsem):
        ids = []
        for d in dests:
            rid, pid = topo.addr(d, core)
            ids.append(DstId(rid=rid, pnc=pid))
        tr = RemoteDMATransfer(dst_ids=ids, dma_engine_mask=mask, remote_sem=rsem, srcs=[src],
                               dsts=[dst for d in dests], alu_op=0)
        g.remote_dma_fused([tr], local_sem=sent[0])
        sent[1] += bits(mask)

    if not is_low:
        wt("g", ld_q)
        send(T.qo[:], T.qf[:], [far], m_cb, T.sem.q_in)
    t_off = [mine[j] for j in takers if j in off]
    t_on = [mine[j] for j in takers if j in on]
    wt("g", ld_kv)
    if is_low:
        send(slot(rr, 0, B), slot(rr, 0, B), t_off, m_sw, T.sem.kv_off)
    wt("g", ld_v)
    if t_off and not is_low:
        send(slot(rr, 0, 2 * B), slot(rr, 0, 2 * B), t_off, m_sw, T.sem.kv_off)
    if t_on:
        send(slot(rr, 0, 2 * B), slot(rr, 0, 2 * B), t_on, m_on, T.sem.kv_on)
    if is_low:
        send(slot(rr, 0, 2 * B), slot(FAR, 0, 2 * B), [far], m_cb, T.sem.kv_far)
        send(slot(rr, B, 2 * B), slot(rr, B, 2 * B), t_off, m_sw, T.sem.v_off)

    def chunk(slots, s, pt, k, data, vdata):
        if rr in slots:
            data = data + [ld_kv]
            vdata = vdata + [ld_v]
        return {"slots": slots, "s": s, "pt": pt, "o": k * CW, "n": len(slots) * B, "data": data, "vdata": vdata, "k": k,
                "S": ev(), "M": ev(), "E": [ev() for j in slots], "T": ev(), "C": ev()}

    def st_S(J, c):
        wt("pe", *(J["qe"] + c["data"]))
        for b, j in enumerate(c["slots"]):
            o = c["s"][:, b * B:(b + 1) * B]
            if J["causal"] and j == rr:
                wt("pe", e_id, e_mb)
                g.tensor.matmul(o, J["q"], slot(j, 0, B), True, False)
                sig(g.tensor.matmul(o, T.ident[:], T.mb[:], False, True), c["S"])
            else:
                sig(g.tensor.matmul(o, J["q"], slot(j, 0, B), True, True), c["S"])

    def st_max(J, c):
        wt("dve", c["S"])
        if len(J["chunks"]) == 1:
            sig(g.vector.tensor_reduce(J["negm"], c["s"][:, 0:c["n"]], X, AluOpType.max, negate=True), J["N"])
        else:
            sig(g.vector.tensor_reduce(T.mx[:, c["k"]:c["k"] + 1], c["s"][:, 0:c["n"]], X, AluOpType.max), c["M"])

    def st_comb(J):
        if len(J["chunks"]) > 1:
            wt("dve", *[c["M"] for c in J["chunks"]])
            k0 = J["chunks"][0]["k"]
            sig(g.vector.tensor_reduce(J["negm"], T.mx[:, k0:k0 + 2], X, AluOpType.max, negate=True), J["N"])

    def st_exp(J, c):
        wt("act", J["N"], c["S"])
        for b in range(len(c["slots"])):
            sig(g.scalar.activation(T.p[:, c["o"] + b * B:c["o"] + (b + 1) * B], c["s"][:, b * B:(b + 1) * B], EXP,
                                    bias=J["negm"], scale=1.0), c["E"][b])

    def st_T(J, c):
        wt("pe", e_id)
        for b in range(len(c["slots"])):
            wt("pe", c["E"][b])
            sig(g.tensor.transpose(c["pt"][:, b * B:(b + 1) * B], T.p[:, c["o"] + b * B:c["o"] + (b + 1) * B], T.ident[:]), c["T"])

    def st_copy(J, c):
        wt("dve", c["T"])
        sig(g.vector.tensor_copy(T.pts[:, c["o"]:c["o"] + c["n"]], c["pt"][:, 0:c["n"]]), c["C"])

    def st_PV(J, c, close):
        wt("pe", c["C"], e_one, *c["vdata"])
        first = c is J["chunks"][0]
        last = c is J["chunks"][-1]
        for b, j in enumerate(c["slots"]):
            sig(g.tensor.matmul(J["out"][:, 0:B + 1], T.pts[:, c["o"] + b * B:c["o"] + (b + 1) * B], slot(j, B, 2 * B + 1),
                                first and b == 0, close and last and b == len(c["slots"]) - 1), J["P"])

    def st_y(J):
        e_r, e_y = ev(), ev()
        wt("dve", J["P"])
        sig(g.vector.reciprocal(T.rcol[:], J["out"][:, B:B + 1]), e_r)
        wt("dve", e_r)
        sig(g.vector.tensor_scalar(T.ysb[:], J["out"][:, 0:B], T.rcol[:], None, AluOpType.mult), e_y)
        wt("sync", e_y)
        sig(g.sync.dma_start(T.y[:], T.ysb[:]), st, 16)
        wt("sync", st)

    C = {"q": T.qo[:], "qe": [ld_q], "causal": True, "out": T.outo, "negm": T.negc[:], "N": ev(), "P": ev()}
    C["chunks"] = [chunk([j for j in on if j <= rr], T.sx, T.pta, 2, [kv_on], [kv_on])]
    second = [j for j in off if j <= rr] + ([] if is_low else [FAR])
    if second:
        C["chunks"].append(chunk(second, T.sy, T.ptb, 3, [kv_off, kv_far], [v_off, kv_far]))
    cc = C["chunks"]

    if is_low:
        F = {"q": T.qf[:], "qe": [q_in], "causal": False, "out": T.outf, "negm": T.nm[:], "N": ev(), "P": ev()}
        F["chunks"] = [chunk([j for j in on if j != rr], T.sa, T.pta, 0, [kv_on], [kv_on]),
                       chunk(off, T.sb, T.ptb, 1, [kv_off], [v_off])]
        fa, fb = F["chunks"]
        st_S(C, cc[0]); st_max(C, cc[0])
        st_S(F, fa); st_max(F, fa)
        st_S(F, fb); st_max(F, fb); st_comb(F)
        wt("g", F["N"])
        send(T.nm[:], T.nmin[:], [far], m_cb, T.sem.m_in)
        for c in cc[1:]:
            st_S(C, c)
        st_exp(F, fa); st_exp(F, fb)
        for c in cc[1:]:
            st_max(C, c)
        st_comb(C)
        st_T(F, fa); st_T(F, fb)
        st_copy(F, fa); st_copy(F, fb)
        st_PV(F, fa, True); st_PV(F, fb, True)
        e_ret = ev()
        wt("dve", F["P"])
        sig(g.vector.tensor_copy(T.ret[:], T.outf[:, 0:B + 1]), e_ret)
        wt("g", e_ret)
        send(T.ret[:], T.retin[:], [far], m_cb, T.sem.p_in)
    else:
        for c in cc:
            st_S(C, c); st_max(C, c)
        st_comb(C)

    for c in cc:
        st_exp(C, c)
    for c in cc:
        st_T(C, c)
    for c in cc:
        st_copy(C, c)
    for c in cc:
        st_PV(C, c, is_low)

    if not is_low:
        e_d, e_e = ev(), ev()
        wt("dve", m_in, C["N"])
        sig(g.vector.tensor_scalar(T.dcol[:], T.negc[:], T.nmin[:], 60.0, AluOpType.subtract, AluOpType.min), e_d)
        wt("act", e_d, e_zm)
        sig(g.scalar.activation(T.ee[:], T.zm[:], EXP, bias=T.dcol[:], scale=1.0), e_e)
        wt("pe", e_e, p_in)
        sig(g.tensor.matmul(T.outo[:, 0:B + 1], T.ee[:], T.retin[:], False, True), C["P"])
    st_y(C)
    wt("g", sent)
